import numpy as np
import ml_dtypes


def mxq(x, axis, fmt="e4m3"):
    dtype, down = {"e4m3": (ml_dtypes.float8_e4m3fn, 7), "e5m2": (ml_dtypes.float8_e5m2, 14)}[fmt]
    v = np.moveaxis(np.asarray(x, np.float32).astype(ml_dtypes.bfloat16).astype(np.float64), axis, -1)
    blocks = v.reshape(v.shape[:-1] + (-1, 32))
    amax = np.abs(blocks).max(-1, keepdims=True)
    byte = np.maximum(np.where(amax > 0, np.frexp(amax)[1] - 1 + 127, 0) - down, 1)
    scale = np.exp2(byte - 127.0)
    codes = (blocks / scale).astype(np.float32).astype(dtype).astype(np.float64)
    return np.moveaxis((codes * scale).reshape(v.shape), -1, axis)


WIDE = False


def mx_kscale(k):
    if not WIDE:
        return np.ones(k)
    levels = np.array([10, -10, 5, -5, 0])
    if k % 512:
        return np.exp2(np.random.permutation(np.resize(levels, k // 32))).repeat(32)
    a = np.empty((k // 512, 16))
    for p in range(k // 512):
        a[p, :8] = np.random.permutation(np.resize(levels, 8))
        for g in range(8):
            far = levels[np.abs(levels - a[p, g]) >= 10]
            a[p, g + 8] = far[np.random.randint(len(far))]
    return np.exp2(a.ravel()).repeat(32)


BF16 = ml_dtypes.bfloat16


def bf(x):
    return np.asarray(x, np.float32).astype(BF16)


def f64(x):
    return np.asarray(x).astype(np.float64)


E2M1 = np.array([0.0, 0.5, 1.0, 1.5, 2.0, 3.0, 4.0, 6.0, -0.0, -0.5, -1.0, -1.5, -2.0, -3.0, -4.0, -6.0])


def pack_weight(w, fmt):
    k, n = w.shape
    w = f64(bf(w)).reshape(k // 32, 32, n)
    amax = np.abs(w).max(1)
    if fmt == "e4m3":
        byte = np.frexp(amax)[1] - 1 + 127 - 7
    else:
        mant, ex = np.frexp(amax / 6.0)
        byte = np.where(mant > 0.5, ex, ex - 1) + 127
    byte = np.clip(np.where(amax > 0, byte, 1), 1, 254)
    scaled = (w * np.exp2(127.0 - byte)[:, None, :]).reshape(k, n).astype(np.float32)
    by_word = np.ascontiguousarray(scaled.reshape(k // 512, 128, 4, n).transpose(0, 1, 3, 2))
    if fmt == "e4m3":
        words = by_word.astype(ml_dtypes.float8_e4m3fn).view(np.uint8)
    else:
        c = by_word.astype(ml_dtypes.float4_e2m1fn).view(np.uint8) & 0xF
        words = c[..., 0::2] | (c[..., 1::2] << 4)
    return np.ascontiguousarray(words), np.ascontiguousarray(byte.astype(np.uint8).reshape(k // 512, 16, n))


def unpack_weight(words, scales, fmt):
    g, p, n, _ = words.shape
    if fmt == "e4m3":
        vals = np.ascontiguousarray(words).view(ml_dtypes.float8_e4m3fn).astype(np.float64)
    else:
        nib = np.empty((g, p, n, 4), np.uint8)
        nib[..., 0::2] = words & 0xF
        nib[..., 1::2] = words >> 4
        vals = E2M1[nib]
    vals = vals * np.repeat(np.exp2(scales.astype(np.float64) - 127.0), 8, axis=1)[..., None]
    return vals.transpose(0, 1, 3, 2).reshape(g * 512, n)
def pack4(w):
    words, scales = pack_weight(w, "e2m1")
    return words.reshape(words.shape[0], 128, -1), scales


def unpack4(words, scales):
    return unpack_weight(words.reshape(words.shape[0], 128, -1, 2), scales, "e2m1")


def planes(Y):
    n, m = Y.shape
    b = f64(bf(Y)).reshape(n // 32, 32, m)
    amax = np.abs(b).max(1)
    byte = np.clip(np.where(amax > 0, np.frexp(amax)[1] - 1 + 127 - 7, 1), 1, 254)
    codes = (b * np.exp2(127.0 - byte)[:, None, :]).reshape(n, m).astype(np.float32).astype(ml_dtypes.float8_e4m3fn).view(np.uint8)
    words = codes.reshape(n // 512, 128, 4, m).transpose(0, 1, 3, 2)
    return np.ascontiguousarray(words), np.ascontiguousarray(byte.astype(np.uint8).reshape(n // 512, 16, m))


M, I, J, N = 2048, 1024, 512, 1024
RHO = 1.0 / 3.0


def setup_inputs():
    rn = np.random.randn
    s = mx_kscale(J)
    t = mx_kscale(I)
    A = 0.07 * np.exp(1.5 * rn(I, J)) / J
    F = np.exp(rn(J, M))
    B = np.exp(0.4 * rn(I, M))
    E = 1.2 * B * np.exp(0.5 * rn(I, M))
    c = RHO / A.sum(axis=0)
    W = 0.3 * np.exp(rn(J, N)) / J
    class_words, class_scales = pack4(W * s[:, None])
    v = np.exp(0.8 * rn(N))
    return {"beam": bf(A * s[None, :] / t[:, None]), "dist": bf(F / s[:, None]),
            "echo": bf(E), "reverb": bf(B / t[:, None]), "step": bf(c / s),
            "class_words": class_words, "class_scales": class_scales, "fish_weight": bf(v)}


def reference(beam, dist, echo, reverb, step, class_words, class_scales, fish_weight):
    A, F, E, B = f64(beam), f64(dist), f64(echo), f64(reverb)
    c, v = f64(step), f64(fish_weight)
    P = B + (mxq(A, 1) @ mxq(F, 0))
    R = E / P
    back = mxq(A, 0).T @ mxq(R, 0)
    F1 = F + F * (c[:, None] * back)
    y = v[None, :] * (mxq(F1, 0).T @ unpack4(class_words, class_scales))
    Y = y.T
    words, scales = planes(Y)
    return y, words, scales

@@ -1,0 +1,365 @@
+from contextlib import ExitStack
+
+import concourse.mybir as mybir
+from concourse.masks import make_identity
+
+M, I, J, N = 2048, 1024, 512, 1024
+FLOPS = 2 * (2 * I * J * M + M * J * N)
+
+F32 = mybir.dt.float32
+BF16 = mybir.dt.bfloat16
+I32 = mybir.dt.int32
+U32 = mybir.dt.uint32
+U8 = mybir.dt.uint8
+FP8X4 = mybir.dt.float8_e4m3fn_x4
+FP4X4 = mybir.dt.float4_e2m1fn_x4
+ACT = mybir.ActivationFunctionType
+ALU = mybir.AluOpType
+
+P = 128
+PACK = 4
+K_PASS = P * PACK
+GROUPS = I // K_PASS
+BANK = 512
+CELLS = 128
+STEPS = M // CELLS
+SPANS = [(0, 256), (256, 512), (512, 1024), (1024, 1536), (1536, 2048)]
+PLANE_CELLS = 512
+RUN = 4
+
+
+def tile_target_strength_em_biomass_k1_kernel(
+    tc, beam, dist, echo, reverb, step, class_words, class_scales, fish_weight, out_0, out_1, out_2
+):
+    nc = tc.nc
+
+    with ExitStack() as ctx:
+        keep = ctx.enter_context(tc.tile_pool(name="keep", bufs=1))
+        work = ctx.enter_context(tc.tile_pool(name="work", bufs=2))
+        psum = ctx.enter_context(tc.psum_pool(name="psum", bufs=1))
+        ctx.enter_context(tc.manual_schedule())
+
+        ident = keep.tile([P, P], F32)
+        make_identity(nc, ident[:])
+        w_scales = keep.tile([P, N], U8, align_bytes=64)
+        nc.gpsimd.memset(w_scales[:].bitcast(I32), 0)
+
+        a_raw = [keep.tile([P, PACK, J], BF16, name="a_raw%d" % g) for g in range(GROUPS)]
+        f_raw = [keep.tile([P, PACK, hi - lo], BF16, name="f_raw%d" % s) for s, (lo, hi) in enumerate(SPANS)]
+        b_raw = [keep.tile([P, GROUPS, PACK, hi - lo], BF16, name="b_raw%d" % s) for s, (lo, hi) in enumerate(SPANS)]
+        e_raw = [keep.tile([P, GROUPS, PACK, hi - lo], BF16, name="e_raw%d" % s) for s, (lo, hi) in enumerate(SPANS)]
+        c_raw = keep.tile([P, PACK], BF16)
+        c_f32 = keep.tile([P, PACK], F32)
+        v_all = keep.tile([P, N], BF16)
+        w_words = keep.tile([P, 2 * N], U8, align_bytes=64)
+
+        def load_rows(dst, src, g, lo, hi):
+            rows = src[g * K_PASS : (g + 1) * K_PASS, lo:hi]
+            nc.sync.dma_start(out=dst, in_=rows.rearrange("(p t) m -> p t m", t=PACK))
+
+        def load_f(s):
+            load_rows(f_raw[s][:], dist, 0, *SPANS[s])
+
+        def load_be(s):
+            for dst, src in ((b_raw, reverb), (e_raw, echo)):
+                for g in range(GROUPS):
+                    load_rows(dst[s][:, g, :, :], src, g, *SPANS[s])
+
+        load_f(0)
+        for g in range(GROUPS):
+            load_rows(a_raw[g][:], beam, g, 0, J)
+        load_be(0)
+        load_f(1)
+        nc.sync.dma_start(out=c_raw[:], in_=step.rearrange("(p t) -> p t", t=PACK))
+        load_be(1)
+        load_f(2)
+        nc.sync.dma_start(out=w_words[:].bitcast(I32), in_=class_words[0].bitcast(I32))
+        for q in range(4):
+            nc.sync.dma_start(
+                out=w_scales[32 * q : 32 * q + 4, :].bitcast(I32),
+                in_=class_scales[0, 4 * q : 4 * q + 4, :].bitcast(I32),
+            )
+        nc.sync.dma_start(out=v_all[:], in_=fish_weight.partition_broadcast(P))
+        load_f(3)
+        load_be(2)
+        load_f(4)
+        load_be(3)
+        load_be(4)
+
+        def quantize(codes, scales, grouped):
+            nc.vector.quantize_mx(out=codes.bitcast(FP8X4), scales=scales, in_=grouped)
+
+        def by_runs_out(grouped):
+            return grouped.rearrange("p (c i t) -> p c t i", i=RUN, t=PACK)
+
+        def by_runs_in(rows):
+            return rows.rearrange("p t (c i) -> p c t i", i=RUN)
+
+        f_grp = [keep.tile([P, (hi - lo) * PACK], BF16, name="f_grp%d" % s, align_bytes=64) for s, (lo, hi) in enumerate(SPANS)]
+        f_codes = [keep.tile([P, hi - lo], U32, name="f_codes%d" % s, align_bytes=64) for s, (lo, hi) in enumerate(SPANS)]
+        f_scales = [keep.tile([P, hi - lo], U8, name="f_scales%d" % s, align_bytes=64) for s, (lo, hi) in enumerate(SPANS)]
+
+        def group_f(s, on_scalar):
+            if on_scalar:
+                nc.scalar.copy(out=by_runs_out(f_grp[s][:]), in_=by_runs_in(f_raw[s][:]))
+            else:
+                nc.vector.tensor_copy(out=by_runs_out(f_grp[s][:]), in_=by_runs_in(f_raw[s][:]))
+
+        def quantize_f(s):
+            quantize(f_codes[s][:], f_scales[s][:], f_grp[s][:])
+
+        at_grp = [keep.tile([P, K_PASS * PACK], BF16, name="at_grp%d" % g, align_bytes=64) for g in range(GROUPS)]
+        at_codes = [keep.tile([P, K_PASS], U32, name="at_codes%d" % g, align_bytes=64) for g in range(GROUPS)]
+        at_scales = [keep.tile([P, K_PASS], U8, name="at_scales%d" % g, align_bytes=64) for g in range(GROUPS)]
+        a_grp = [keep.tile([P, J * PACK], BF16, name="a_grp%d" % g, align_bytes=64) for g in range(GROUPS)]
+        a_codes = [keep.tile([P, J], U32, name="a_codes%d" % g, align_bytes=64) for g in range(GROUPS)]
+        a_scales = [keep.tile([P, J], U8, name="a_scales%d" % g, align_bytes=64) for g in range(GROUPS)]
+
+        def turn_a(g):
+            for half in range(2):
+                bank = psum.tile([P, 2, 2, P], F32, tag=("y%d" if half == 0 else "yt%d") % g, name="at_ps")
+                for tt in range(2):
+                    pairs = a_raw[g][:, 2 * half + tt, :].bitcast(F32)
+                    for u in range(2):
+                        nc.tensor.transpose(bank[:, tt, u, :], pairs[:, u : 2 * P : 2], ident[:])
+                dst = at_grp[g][:, half * 1024 : (half + 1) * 1024].bitcast(F32)
+                nc.scalar.copy(
+                    out=dst.rearrange("p (t m u) -> p t m u", t=2, u=2),
+                    in_=bank[:].rearrange("p t u m -> p t m u"),
+                )
+
+        def group_a(g):
+            nc.vector.tensor_copy(
+                out=a_grp[g][:].rearrange("p (s m t) -> p s m t", s=PACK, t=PACK),
+                in_=a_raw[g][:].rearrange("p t (m s) -> p s m t", s=PACK),
+            )
+
+        def span_of(c):
+            s = [k for k, (lo, hi) in enumerate(SPANS) if lo <= c * CELLS < hi][0]
+            return s, slice(c * CELLS - SPANS[s][0], (c + 1) * CELLS - SPANS[s][0])
+
+        p_ps, d_ps, y_ps, yt_ps = {}, {}, {}, {}
+        p_sb, inv, sgn, es, gain, r_q, f1_q, f1_grp, r_grp, y_sb, y_grp = {}, {}, {}, {}, {}, {}, {}, {}, {}, {}, {}
+        y_codes = {}
+        y_scales = keep.tile([P, GROUPS, M], U8, align_bytes=64)
+
+        def predict(c, g):
+            s, cols = span_of(c)
+            p_ps[c, g] = psum.tile([P, PACK, CELLS], F32, tag="p%d" % g, name="p_ps")
+            for t in range(PACK):
+                ch = slice(t * P, (t + 1) * P)
+                nc.tensor.matmul_mx(
+                    out=p_ps[c, g][:, t, :],
+                    lhsT=at_codes[g][:, ch].bitcast(FP8X4),
+                    lhsT_scale=at_scales[g][:, ch],
+                    rhs=f_codes[s][:, cols].bitcast(FP8X4),
+                    rhs_scale=f_scales[s][:, cols],
+                    start=True,
+                    stop=True,
+                )
+
+        def add_background(c):
+            s, cols = span_of(c)
+            p_sb[c] = work.tile([P, PACK, GROUPS, CELLS], F32, tag="p_sb", name="p_sb")
+            for g in range(GROUPS):
+                nc.vector.tensor_tensor(out=p_sb[c][:, :, g, :], in0=p_ps[c, g][:], in1=b_raw[s][:, g, :, cols], op=ALU.add)
+
+        def invert(c):
+            flat = p_sb[c][:].rearrange("p t g m -> p (t g m)")
+            inv[c] = work.tile([P, PACK * GROUPS * CELLS], F32, tag="inv", name="inv")
+            sgn[c] = work.tile([P, PACK * GROUPS * CELLS], BF16, tag="sgn", name="sgn")
+            nc.scalar.activation(out=inv[c][:], in_=flat, func=ACT.Abs_reciprocal_sqrt)
+            nc.scalar.activation(out=sgn[c][:], in_=flat, func=ACT.Sign)
+            nc.scalar.activation(out=inv[c][:], in_=inv[c][:], func=ACT.Square)
+
+        def sign_echo(c):
+            s, cols = span_of(c)
+            es[c] = work.tile([P, PACK, GROUPS, CELLS], BF16, tag="es", name="es")
+            nc.vector.tensor_tensor(
+                out=es[c][:],
+                in0=e_raw[s][:, :, :, cols].rearrange("p g t m -> p t g m"),
+                in1=sgn[c][:].rearrange("p (t g m) -> p t g m", t=PACK, g=GROUPS),
+                op=ALU.mult,
+            )
+
+        def ratio(c):
+            r_grp[c] = work.tile([P, GROUPS * CELLS * PACK], BF16, tag="r_grp", name="r_grp", align_bytes=64)
+            nc.vector.tensor_tensor(
+                out=by_runs_out(r_grp[c][:]),
+                in0=by_runs_in(inv[c][:].rearrange("p (t x) -> p t x", t=PACK)),
+                in1=by_runs_in(es[c][:].rearrange("p t g m -> p t (g m)")),
+                op=ALU.mult,
+            )
+
+        def quantize_ratio(c):
+            codes = work.tile([P, GROUPS * CELLS], U32, tag="r_codes", name="r_codes", align_bytes=64)
+            scales = work.tile([P, GROUPS * CELLS], U8, tag="r_scales", name="r_scales", align_bytes=64)
+            quantize(codes[:], scales[:], r_grp[c][:])
+            r_q[c] = (codes, scales)
+
+        def back_project(c):
+            codes, scales = r_q[c]
+            d_ps[c] = psum.tile([P, PACK, CELLS], F32, tag="d", name="d_ps", bufs=2)
+            for t in range(PACK):
+                bins = slice(t * P, (t + 1) * P)
+                for g in range(GROUPS):
+                    cols = slice(g * CELLS, (g + 1) * CELLS)
+                    nc.tensor.matmul_mx(
+                        out=d_ps[c][:, t, :],
+                        lhsT=a_codes[g][:, bins].bitcast(FP8X4),
+                        lhsT_scale=a_scales[g][:, bins],
+                        rhs=codes[:, cols].bitcast(FP8X4),
+                        rhs_scale=scales[:, cols],
+                        start=(g == 0),
+                        stop=(g == GROUPS - 1),
+                    )
+
+        def step_gain(c):
+            gain[c] = work.tile([P, PACK, CELLS], F32, tag="gain", name="gain")
+            for t in range(PACK):
+                nc.scalar.activation(
+                    out=gain[c][:, t, :], in_=d_ps[c][:, t, :], func=ACT.Copy, scale=c_f32[:, t : t + 1], bias=1.0
+                )
+
+        def update(c):
+            s, cols = span_of(c)
+            f1_grp[c] = work.tile([P, CELLS * PACK], BF16, tag="f1_grp", name="f1_grp", align_bytes=64)
+            nc.vector.tensor_tensor(
+                out=by_runs_out(f1_grp[c][:]),
+                in0=by_runs_in(gain[c][:]),
+                in1=by_runs_out(f_grp[s][:, cols.start * PACK : cols.stop * PACK]),
+                op=ALU.mult,
+            )
+
+        def quantize_update(c):
+            codes = work.tile([P, CELLS], U32, tag="f1_codes", name="f1_codes", align_bytes=64)
+            scales = work.tile([P, CELLS], U8, tag="f1_scales", name="f1_scales", align_bytes=64)
+            quantize(codes[:], scales[:], f1_grp[c][:])
+            f1_q[c] = (codes, scales)
+
+        def classify(c):
+            codes, scales = f1_q[c]
+            for h in range(GROUPS):
+                y_ps[c, h] = psum.tile([P, BANK], F32, tag="y%d" % h, name="y_ps")
+                nc.tensor.matmul_mx(
+                    out=y_ps[c, h][:],
+                    lhsT=codes[:].bitcast(FP8X4),
+                    lhsT_scale=scales[:],
+                    rhs=w_words[:, 2 * h * BANK : 2 * (h + 1) * BANK].bitcast(FP4X4),
+                    rhs_scale=w_scales[:, h * BANK : (h + 1) * BANK],
+                    start=True,
+                    stop=True,
+                )
+
+        def weigh(c):
+            y_sb[c] = work.tile([P, N], F32, tag="y_sb", name="y_sb", bufs=3)
+            for h in range(GROUPS):
+                cols = slice(h * BANK, (h + 1) * BANK)
+                nc.vector.tensor_tensor(out=y_sb[c][:, cols], in0=y_ps[c, h][:], in1=v_all[:, cols], op=ALU.mult)
+            nc.sync.dma_start(out=out_0[c * CELLS : (c + 1) * CELLS, :], in_=y_sb[c][:])
+
+        def turn_y(c):
+            for g in range(GROUPS):
+                yt_ps[c, g] = psum.tile([P, PACK, CELLS], F32, tag="yt%d" % g, name="yt_ps")
+                for t in range(PACK):
+                    nc.tensor.transpose(
+                        yt_ps[c, g][:, t, :], y_sb[c][:, g * K_PASS + t : (g + 1) * K_PASS : PACK], ident[:]
+                    )
+
+        def round_y(c):
+            y_grp[c] = work.tile([P, GROUPS, CELLS * PACK], BF16, tag="y_grp", name="y_grp", align_bytes=64)
+            for g in range(GROUPS):
+                nc.scalar.copy(
+                    out=y_grp[c][:, g, :].rearrange("p (m t) -> p m t", t=PACK),
+                    in_=yt_ps[c, g][:].rearrange("p t m -> p m t"),
+                )
+
+        def quantize_y(c):
+            per = PLANE_CELLS // CELLS
+            b, k = divmod(c, per)
+            if k == 0:
+                y_codes[b] = work.tile([P, GROUPS, PLANE_CELLS], U32, tag="y_codes", name="y_codes", align_bytes=64)
+            for g in range(GROUPS):
+                quantize(
+                    y_codes[b][:, g, k * CELLS : (k + 1) * CELLS],
+                    y_scales[:, g, c * CELLS : (c + 1) * CELLS],
+                    y_grp[c][:, g, :],
+                )
+            if k == per - 1:
+                cells = slice(b * PLANE_CELLS, (b + 1) * PLANE_CELLS)
+                nc.sync.dma_start(
+                    out=out_1[:, :, cells, :].rearrange("g p m t -> p g (m t)").bitcast(I32),
+                    in_=y_codes[b][:].bitcast(I32),
+                )
+            if c in (STEPS - per - 1, STEPS - 1):
+                cells = slice(0, M - PLANE_CELLS) if c < STEPS - 1 else slice(M - PLANE_CELLS, M)
+                for q in range(4):
+                    nc.sync.dma_start(
+                        out=out_2[:, 4 * q : 4 * q + 4, cells].rearrange("g r m -> r g m").bitcast(I32),
+                        in_=y_scales[32 * q : 32 * q + 4, :, cells].bitcast(I32),
+                    )
+
+        group_f(0, False)
+        turn_a(0)
+        group_a(0)
+        quantize_f(0)
+        turn_a(1)
+        quantize(at_codes[0][:], at_scales[0][:], at_grp[0][:])
+        predict(0, 0)
+        quantize(a_codes[0][:], a_scales[0][:], a_grp[0][:])
+        quantize(at_codes[1][:], at_scales[1][:], at_grp[1][:])
+        predict(0, 1)
+
+        def live(c):
+            return 0 <= c < STEPS
+
+        for i in range(STEPS + 4):
+            if live(i - 3):
+                classify(i - 3)
+            if live(i - 2):
+                back_project(i - 2)
+            if live(i - 4):
+                round_y(i - 4)
+            if live(i):
+                add_background(i)
+            if live(i - 2):
+                step_gain(i - 2)
+            if live(i - 3):
+                weigh(i - 3)
+            if i == 0:
+                group_f(1, False)
+                group_a(1)
+                quantize_f(1)
+                nc.vector.tensor_copy(out=c_f32[:], in_=c_raw[:])
+                quantize(a_codes[1][:], a_scales[1][:], a_grp[1][:])
+            if i == 2:
+                quantize_f(2)
+            if i == 5:
+                quantize_f(3)
+            if i == 8:
+                group_f(4, False)
+            if i == 9:
+                quantize_f(4)
+            if live(i + 1):
+                for g in range(GROUPS):
+                    predict(i + 1, g)
+            if live(i - 3):
+                turn_y(i - 3)
+            if live(i):
+                invert(i)
+            if i == 1:
+                group_f(2, True)
+            if i == 3:
+                group_f(3, True)
+            if live(i - 2):
+                update(i - 2)
+            if live(i - 1):
+                sign_echo(i - 1)
+            if live(i - 2):
+                quantize_update(i - 2)
+            if live(i - 1):
+                ratio(i - 1)
+            if live(i - 4):
+                quantize_y(i - 4)
+            if live(i - 1):
+                quantize_ratio(i - 1)

@@ -26,6 +26,11 @@ STEPS = M // CELLS
 SPANS = [(0, 256), (256, 512), (512, 1024), (1024, 1536), (1536, 2048)]
 PLANE_CELLS = 512
 RUN = 4
+R_COLS = GROUPS * CELLS
+POOL_COLS = 160
+SIGN_SPLIT = 768
+PLANE_SPANS = [(0, 512), (512, 1024), (1024, 1536), (1536, 1920), (1920, 2048)]
+SCALE_SPANS = [(0, 1536), (1536, 1920), (1920, 2048)]
 
 
 def tile_target_strength_em_biomass_k1_kernel(
@@ -60,19 +65,25 @@ def tile_target_strength_em_biomass_k1_kernel(
         def load_f(s):
             load_rows(f_raw[s][:], dist, 0, *SPANS[s])
 
-        def load_be(s):
-            for dst, src in ((b_raw, reverb), (e_raw, echo)):
-                for g in range(GROUPS):
-                    load_rows(dst[s][:, g, :, :], src, g, *SPANS[s])
+        def load_pair(dst, src, s):
+            for g in range(GROUPS):
+                load_rows(dst[s][:, g, :, :], src, g, *SPANS[s])
 
+        for half in range(2):
+            nc.sync.dma_start(
+                out=a_raw[0][:, 2 * half : 2 * half + 2, :],
+                in_=beam[0:K_PASS, :].rearrange("(p t) j -> p t j", t=PACK)[:, 2 * half : 2 * half + 2, :],
+            )
         load_f(0)
-        for g in range(GROUPS):
-            load_rows(a_raw[g][:], beam, g, 0, J)
-        load_be(0)
+        load_rows(a_raw[1][:], beam, 1, 0, J)
+        load_pair(b_raw, reverb, 0)
         load_f(1)
-        nc.sync.dma_start(out=c_raw[:], in_=step.rearrange("(p t) -> p t", t=PACK))
-        load_be(1)
         load_f(2)
+        load_pair(e_raw, echo, 0)
+        nc.sync.dma_start(out=c_raw[:], in_=step.rearrange("(p t) -> p t", t=PACK))
+        load_pair(b_raw, reverb, 1)
+        load_f(3)
+        load_pair(e_raw, echo, 1)
         nc.sync.dma_start(out=w_words[:].bitcast(I32), in_=class_words[0].bitcast(I32))
         for q in range(4):
             nc.sync.dma_start(
@@ -80,11 +91,12 @@ def tile_target_strength_em_biomass_k1_kernel(
                 in_=class_scales[0, 4 * q : 4 * q + 4, :].bitcast(I32),
             )
         nc.sync.dma_start(out=v_all[:], in_=fish_weight.partition_broadcast(P))
-        load_f(3)
-        load_be(2)
+        load_pair(b_raw, reverb, 2)
+        load_pair(e_raw, echo, 2)
         load_f(4)
-        load_be(3)
-        load_be(4)
+        for s in (3, 4):
+            load_pair(b_raw, reverb, s)
+            load_pair(e_raw, echo, s)
 
         def quantize(codes, scales, grouped):
             nc.vector.quantize_mx(out=codes.bitcast(FP8X4), scales=scales, in_=grouped)
@@ -99,11 +111,8 @@ def tile_target_strength_em_biomass_k1_kernel(
         f_codes = [keep.tile([P, hi - lo], U32, name="f_codes%d" % s, align_bytes=64) for s, (lo, hi) in enumerate(SPANS)]
         f_scales = [keep.tile([P, hi - lo], U8, name="f_scales%d" % s, align_bytes=64) for s, (lo, hi) in enumerate(SPANS)]
 
-        def group_f(s, on_scalar):
-            if on_scalar:
-                nc.scalar.copy(out=by_runs_out(f_grp[s][:]), in_=by_runs_in(f_raw[s][:]))
-            else:
-                nc.vector.tensor_copy(out=by_runs_out(f_grp[s][:]), in_=by_runs_in(f_raw[s][:]))
+        def group_f(s):
+            nc.vector.tensor_copy(out=by_runs_out(f_grp[s][:]), in_=by_runs_in(f_raw[s][:]))
 
         def quantize_f(s):
             quantize(f_codes[s][:], f_scales[s][:], f_grp[s][:])
@@ -158,19 +167,33 @@ def tile_target_strength_em_biomass_k1_kernel(
                     stop=True,
                 )
 
-        def add_background(c):
+        def add_background(c, g):
             s, cols = span_of(c)
-            p_sb[c] = work.tile([P, PACK, GROUPS, CELLS], F32, tag="p_sb", name="p_sb")
-            for g in range(GROUPS):
-                nc.vector.tensor_tensor(out=p_sb[c][:, :, g, :], in0=p_ps[c, g][:], in1=b_raw[s][:, g, :, cols], op=ALU.add)
+            if g == 0:
+                p_sb[c] = work.tile([P, PACK, GROUPS, CELLS], F32, tag="p_sb", name="p_sb")
+            nc.vector.tensor_tensor(out=p_sb[c][:, :, g, :], in0=p_ps[c, g][:], in1=b_raw[s][:, g, :, cols], op=ALU.add)
 
         def invert(c):
             flat = p_sb[c][:].rearrange("p t g m -> p (t g m)")
-            inv[c] = work.tile([P, PACK * GROUPS * CELLS], F32, tag="inv", name="inv")
-            sgn[c] = work.tile([P, PACK * GROUPS * CELLS], BF16, tag="sgn", name="sgn")
-            nc.scalar.activation(out=inv[c][:], in_=flat, func=ACT.Abs_reciprocal_sqrt)
-            nc.scalar.activation(out=sgn[c][:], in_=flat, func=ACT.Sign)
+            inv[c] = work.tile([P, PACK * R_COLS], F32, tag="inv", name="inv")
+            sgn[c] = work.tile([P, PACK * R_COLS], BF16, tag="sgn", name="sgn")
+            nc.scalar.activation(out=inv[c][:, :SIGN_SPLIT], in_=flat[:, :SIGN_SPLIT], func=ACT.Abs_reciprocal_sqrt)
+            nc.scalar.activation(
+                out=inv[c][:, SIGN_SPLIT:], in_=flat[:, SIGN_SPLIT:], func=ACT.Abs_reciprocal_sqrt, scale=0.5
+            )
             nc.scalar.activation(out=inv[c][:], in_=inv[c][:], func=ACT.Square)
+            nc.scalar.activation(out=sgn[c][:, :SIGN_SPLIT], in_=flat[:, :SIGN_SPLIT], func=ACT.Sign)
+
+        def half_sign(c):
+            flat = p_sb[c][:].rearrange("p t g m -> p (t g m)")
+            nc.vector.tensor_scalar(
+                out=sgn[c][:, SIGN_SPLIT:],
+                in0=flat[:, SIGN_SPLIT:],
+                scalar1=0.0,
+                scalar2=0.5,
+                op0=ALU.is_ge,
+                op1=ALU.subtract,
+            )
 
         def sign_echo(c):
             s, cols = span_of(c)
@@ -182,12 +205,20 @@ def tile_target_strength_em_biomass_k1_kernel(
                 op=ALU.mult,
             )
 
+        def ratio_pool(c):
+            r_grp[c] = work.tile([P, R_COLS * PACK], BF16, tag="r_grp", name="r_grp", align_bytes=64)
+            nc.gpsimd.tensor_tensor(
+                out=r_grp[c][:, : POOL_COLS * PACK].rearrange("p (x t) -> p x t", t=PACK),
+                in0=inv[c][:].rearrange("p (t x) -> p x t", t=PACK)[:, :POOL_COLS, :],
+                in1=es[c][:].rearrange("p t g m -> p (g m) t")[:, :POOL_COLS, :],
+                op=ALU.mult,
+            )
+
         def ratio(c):
-            r_grp[c] = work.tile([P, GROUPS * CELLS * PACK], BF16, tag="r_grp", name="r_grp", align_bytes=64)
             nc.vector.tensor_tensor(
-                out=by_runs_out(r_grp[c][:]),
-                in0=by_runs_in(inv[c][:].rearrange("p (t x) -> p t x", t=PACK)),
-                in1=by_runs_in(es[c][:].rearrange("p t g m -> p t (g m)")),
+                out=by_runs_out(r_grp[c][:, POOL_COLS * PACK :]),
+                in0=by_runs_in(inv[c][:].rearrange("p (t x) -> p t x", t=PACK)[:, :, POOL_COLS:]),
+                in1=by_runs_in(es[c][:].rearrange("p t g m -> p t (g m)")[:, :, POOL_COLS:]),
                 op=ALU.mult,
             )
 
@@ -285,61 +316,50 @@ def tile_target_strength_em_biomass_k1_kernel(
                     y_scales[:, g, c * CELLS : (c + 1) * CELLS],
                     y_grp[c][:, g, :],
                 )
-            if k == per - 1:
-                cells = slice(b * PLANE_CELLS, (b + 1) * PLANE_CELLS)
-                nc.sync.dma_start(
-                    out=out_1[:, :, cells, :].rearrange("g p m t -> p g (m t)").bitcast(I32),
-                    in_=y_codes[b][:].bitcast(I32),
-                )
-            if c in (STEPS - per - 1, STEPS - 1):
-                cells = slice(0, M - PLANE_CELLS) if c < STEPS - 1 else slice(M - PLANE_CELLS, M)
-                for q in range(4):
+            for lo, hi in PLANE_SPANS:
+                if hi == (c + 1) * CELLS:
                     nc.sync.dma_start(
-                        out=out_2[:, 4 * q : 4 * q + 4, cells].rearrange("g r m -> r g m").bitcast(I32),
-                        in_=y_scales[32 * q : 32 * q + 4, :, cells].bitcast(I32),
+                        out=out_1[:, :, lo:hi, :].rearrange("g p m t -> p g (m t)").bitcast(I32),
+                        in_=y_codes[b][:, :, lo - b * PLANE_CELLS : hi - b * PLANE_CELLS].bitcast(I32),
                     )
+            for lo, hi in SCALE_SPANS:
+                if hi == (c + 1) * CELLS:
+                    for q in range(4):
+                        nc.sync.dma_start(
+                            out=out_2[:, 4 * q : 4 * q + 4, lo:hi].rearrange("g r m -> r g m").bitcast(I32),
+                            in_=y_scales[32 * q : 32 * q + 4, :, lo:hi].bitcast(I32),
+                        )
 
-        group_f(0, False)
         turn_a(0)
+        turn_a(1)
+        group_f(0)
         group_a(0)
         quantize_f(0)
-        turn_a(1)
+        quantize(a_codes[0][:], a_scales[0][:], a_grp[0][:])
         quantize(at_codes[0][:], at_scales[0][:], at_grp[0][:])
         predict(0, 0)
-        quantize(a_codes[0][:], a_scales[0][:], a_grp[0][:])
+        group_a(1)
+        add_background(0, 0)
         quantize(at_codes[1][:], at_scales[1][:], at_grp[1][:])
         predict(0, 1)
+        quantize(a_codes[1][:], a_scales[1][:], a_grp[1][:])
 
         def live(c):
             return 0 <= c < STEPS
 
         for i in range(STEPS + 4):
-            if live(i - 3):
-                classify(i - 3)
-            if live(i - 2):
-                back_project(i - 2)
             if live(i - 4):
                 round_y(i - 4)
-            if live(i):
-                add_background(i)
             if live(i - 2):
                 step_gain(i - 2)
+            if live(i - 1):
+                ratio_pool(i - 1)
+            if live(i):
+                for g in range(GROUPS):
+                    if (i, g) != (0, 0):
+                        add_background(i, g)
             if live(i - 3):
                 weigh(i - 3)
-            if i == 0:
-                group_f(1, False)
-                group_a(1)
-                quantize_f(1)
-                nc.vector.tensor_copy(out=c_f32[:], in_=c_raw[:])
-                quantize(a_codes[1][:], a_scales[1][:], a_grp[1][:])
-            if i == 2:
-                quantize_f(2)
-            if i == 5:
-                quantize_f(3)
-            if i == 8:
-                group_f(4, False)
-            if i == 9:
-                quantize_f(4)
             if live(i + 1):
                 for g in range(GROUPS):
                     predict(i + 1, g)
@@ -347,19 +367,34 @@ def tile_target_strength_em_biomass_k1_kernel(
                 turn_y(i - 3)
             if live(i):
                 invert(i)
-            if i == 1:
-                group_f(2, True)
-            if i == 3:
-                group_f(3, True)
-            if live(i - 2):
-                update(i - 2)
-            if live(i - 1):
-                sign_echo(i - 1)
-            if live(i - 2):
-                quantize_update(i - 2)
+            if i == 0:
+                group_f(1)
+                group_f(2)
+                quantize_f(1)
+                nc.vector.tensor_copy(out=c_f32[:], in_=c_raw[:])
             if live(i - 1):
                 ratio(i - 1)
-            if live(i - 4):
-                quantize_y(i - 4)
+            if live(i - 2):
+                update(i - 2)
+            if i == 1:
+                quantize_f(2)
             if live(i - 1):
                 quantize_ratio(i - 1)
+                back_project(i - 1)
+            if live(i - 2):
+                quantize_update(i - 2)
+                classify(i - 2)
+            if i == 1:
+                group_f(3)
+            if i == 2:
+                quantize_f(3)
+            if i == 6:
+                group_f(4)
+            if i == 7:
+                quantize_f(4)
+            if live(i):
+                half_sign(i)
+            if live(i - 4):
+                quantize_y(i - 4)
+            if live(i):
+                sign_echo(i)

@@ -21,16 +21,16 @@ PACK = 4
 K_PASS = P * PACK
 GROUPS = I // K_PASS
 BANK = 512
-CELLS = 128
-STEPS = M // CELLS
-SPANS = [(0, 256), (256, 512), (512, 1024), (1024, 1536), (1536, 2048)]
-PLANE_CELLS = 512
 RUN = 4
-R_COLS = GROUPS * CELLS
-POOL_COLS = 160
-SIGN_SPLIT = 768
-PLANE_SPANS = [(0, 512), (512, 1024), (1024, 1536), (1536, 1920), (1920, 2048)]
-SCALE_SPANS = [(0, 1536), (1536, 1920), (1920, 2048)]
+WIDTHS = [128, 128, 256, 256, 256, 256, 256, 256, 128, 128]
+STARTS = [sum(WIDTHS[:c]) for c in range(len(WIDTHS) + 1)]
+STEPS = len(WIDTHS)
+SPANS = [(0, 256), (256, 512), (512, 1024), (1024, 1536), (1536, 2048)]
+F_PART = 256
+F_PARTS_ON_VECTOR = (0, 3, 4, 5)
+PLANE_CELLS = 512
+WORD_SPANS = [(0, 512), (512, 1024), (1024, 1536), (1536, 1920), (1920, 2048)]
+SCALE_SPANS = [(0, 1536), (1536, 2048)]
 
 
 def tile_target_strength_em_biomass_k1_kernel(
@@ -49,93 +49,108 @@ def tile_target_strength_em_biomass_k1_kernel(
         w_scales = keep.tile([P, N], U8, align_bytes=64)
         nc.gpsimd.memset(w_scales[:].bitcast(I32), 0)
 
-        a_raw = [keep.tile([P, PACK, J], BF16, name="a_raw%d" % g) for g in range(GROUPS)]
+        a_raw = [work.tile([P, PACK, J], BF16, name="a_raw%d" % g, tag="y_sb", bufs=4) for g in range(GROUPS)]
         f_raw = [keep.tile([P, PACK, hi - lo], BF16, name="f_raw%d" % s) for s, (lo, hi) in enumerate(SPANS)]
-        b_raw = [keep.tile([P, GROUPS, PACK, hi - lo], BF16, name="b_raw%d" % s) for s, (lo, hi) in enumerate(SPANS)]
-        e_raw = [keep.tile([P, GROUPS, PACK, hi - lo], BF16, name="e_raw%d" % s) for s, (lo, hi) in enumerate(SPANS)]
+        b_raw, e_raw = {}, {}
         c_raw = keep.tile([P, PACK], BF16)
         c_f32 = keep.tile([P, PACK], F32)
         v_all = keep.tile([P, N], BF16)
         w_words = keep.tile([P, 2 * N], U8, align_bytes=64)
 
-        def load_rows(dst, src, g, lo, hi):
-            rows = src[g * K_PASS : (g + 1) * K_PASS, lo:hi]
-            nc.sync.dma_start(out=dst, in_=rows.rearrange("(p t) m -> p t m", t=PACK))
+        def rows_of(src, g, lo, hi):
+            return src[g * K_PASS : (g + 1) * K_PASS, lo:hi].rearrange("(p t) m -> p t m", t=PACK)
 
         def load_f(s):
-            load_rows(f_raw[s][:], dist, 0, *SPANS[s])
+            nc.sync.dma_start(out=f_raw[s][:], in_=rows_of(dist, 0, *SPANS[s]))
 
-        def load_pair(dst, src, s):
+        def load_a(g):
+            for half in range(2):
+                slots = slice(2 * half, 2 * half + 2)
+                nc.sync.dma_start(out=a_raw[g][:, slots, :], in_=rows_of(beam, g, 0, J)[:, slots, :])
+
+        def load_channels(dst, src, tag, s):
+            lo, hi = SPANS[s]
+            dst[s] = work.tile([P, GROUPS, PACK, hi - lo], BF16, name=tag, tag=tag, bufs=3)
             for g in range(GROUPS):
-                load_rows(dst[s][:, g, :, :], src, g, *SPANS[s])
+                nc.sync.dma_start(out=dst[s][:, g, :, :], in_=rows_of(src, g, lo, hi))
 
-        for half in range(2):
-            nc.sync.dma_start(
-                out=a_raw[0][:, 2 * half : 2 * half + 2, :],
-                in_=beam[0:K_PASS, :].rearrange("(p t) j -> p t j", t=PACK)[:, 2 * half : 2 * half + 2, :],
-            )
+        load_a(0)
         load_f(0)
-        load_rows(a_raw[1][:], beam, 1, 0, J)
-        load_pair(b_raw, reverb, 0)
+        load_a(1)
+        load_channels(b_raw, reverb, "b_raw", 0)
         load_f(1)
-        load_f(2)
-        load_pair(e_raw, echo, 0)
+        load_channels(e_raw, echo, "e_raw", 0)
         nc.sync.dma_start(out=c_raw[:], in_=step.rearrange("(p t) -> p t", t=PACK))
-        load_pair(b_raw, reverb, 1)
-        load_f(3)
-        load_pair(e_raw, echo, 1)
+        load_f(2)
+        load_channels(b_raw, reverb, "b_raw", 1)
+        load_channels(e_raw, echo, "e_raw", 1)
         nc.sync.dma_start(out=w_words[:].bitcast(I32), in_=class_words[0].bitcast(I32))
         for q in range(4):
             nc.sync.dma_start(
                 out=w_scales[32 * q : 32 * q + 4, :].bitcast(I32),
                 in_=class_scales[0, 4 * q : 4 * q + 4, :].bitcast(I32),
             )
+        load_f(3)
         nc.sync.dma_start(out=v_all[:], in_=fish_weight.partition_broadcast(P))
-        load_pair(b_raw, reverb, 2)
-        load_pair(e_raw, echo, 2)
+        load_channels(b_raw, reverb, "b_raw", 2)
+        load_channels(e_raw, echo, "e_raw", 2)
         load_f(4)
         for s in (3, 4):
-            load_pair(b_raw, reverb, s)
-            load_pair(e_raw, echo, s)
+            load_channels(b_raw, reverb, "b_raw", s)
+            load_channels(e_raw, echo, "e_raw", s)
 
         def quantize(codes, scales, grouped):
             nc.vector.quantize_mx(out=codes.bitcast(FP8X4), scales=scales, in_=grouped)
 
-        def by_runs_out(grouped):
+        def runs_of_words(grouped):
             return grouped.rearrange("p (c i t) -> p c t i", i=RUN, t=PACK)
 
-        def by_runs_in(rows):
+        def runs_of_rows(rows):
             return rows.rearrange("p t (c i) -> p c t i", i=RUN)
 
-        f_grp = [keep.tile([P, (hi - lo) * PACK], BF16, name="f_grp%d" % s, align_bytes=64) for s, (lo, hi) in enumerate(SPANS)]
-        f_codes = [keep.tile([P, hi - lo], U32, name="f_codes%d" % s, align_bytes=64) for s, (lo, hi) in enumerate(SPANS)]
-        f_scales = [keep.tile([P, hi - lo], U8, name="f_scales%d" % s, align_bytes=64) for s, (lo, hi) in enumerate(SPANS)]
+        def span_of(lo, width):
+            s = [k for k, (first, last) in enumerate(SPANS) if first <= lo < last][0]
+            return s, slice(lo - SPANS[s][0], lo + width - SPANS[s][0])
 
-        def group_f(s):
-            nc.vector.tensor_copy(out=by_runs_out(f_grp[s][:]), in_=by_runs_in(f_raw[s][:]))
+        f_grp = keep.tile([P, M * PACK], BF16, align_bytes=64)
+        f_codes = keep.tile([P, M], U32, align_bytes=64)
+        f_scales = keep.tile([P, M], U8, align_bytes=64)
 
-        def quantize_f(s):
-            quantize(f_codes[s][:], f_scales[s][:], f_grp[s][:])
+        def group_f(u):
+            s, cols = span_of(u * F_PART, F_PART)
+            dst = runs_of_words(f_grp[:, u * F_PART * PACK : (u + 1) * F_PART * PACK])
+            src = runs_of_rows(f_raw[s][:, :, cols])
+            if u in F_PARTS_ON_VECTOR:
+                nc.vector.tensor_copy(out=dst, in_=src)
+            else:
+                nc.scalar.copy(out=dst, in_=src)
 
-        at_grp = [keep.tile([P, K_PASS * PACK], BF16, name="at_grp%d" % g, align_bytes=64) for g in range(GROUPS)]
-        at_codes = [keep.tile([P, K_PASS], U32, name="at_codes%d" % g, align_bytes=64) for g in range(GROUPS)]
-        at_scales = [keep.tile([P, K_PASS], U8, name="at_scales%d" % g, align_bytes=64) for g in range(GROUPS)]
-        a_grp = [keep.tile([P, J * PACK], BF16, name="a_grp%d" % g, align_bytes=64) for g in range(GROUPS)]
-        a_codes = [keep.tile([P, J], U32, name="a_codes%d" % g, align_bytes=64) for g in range(GROUPS)]
-        a_scales = [keep.tile([P, J], U8, name="a_scales%d" % g, align_bytes=64) for g in range(GROUPS)]
+        def quantize_f(u):
+            cells = slice(u * F_PART, (u + 1) * F_PART)
+            quantize(f_codes[:, cells], f_scales[:, cells], f_grp[:, u * F_PART * PACK : (u + 1) * F_PART * PACK])
 
-        def turn_a(g):
-            for half in range(2):
-                bank = psum.tile([P, 2, 2, P], F32, tag=("y%d" if half == 0 else "yt%d") % g, name="at_ps")
-                for tt in range(2):
-                    pairs = a_raw[g][:, 2 * half + tt, :].bitcast(F32)
-                    for u in range(2):
-                        nc.tensor.transpose(bank[:, tt, u, :], pairs[:, u : 2 * P : 2], ident[:])
-                dst = at_grp[g][:, half * 1024 : (half + 1) * 1024].bitcast(F32)
-                nc.scalar.copy(
-                    out=dst.rearrange("p (t m u) -> p t m u", t=2, u=2),
-                    in_=bank[:].rearrange("p t u m -> p t m u"),
-                )
+        at_grp = [work.tile([P, K_PASS * PACK], BF16, name="at_grp%d" % g, tag="y_grp", align_bytes=64) for g in range(GROUPS)]
+        at_codes = keep.tile([P, I], U32, align_bytes=64)
+        at_scales = keep.tile([P, I], U8, align_bytes=64)
+        a_grp = [work.tile([P, J * PACK], BF16, name="a_grp%d" % g, tag="gain", align_bytes=64) for g in range(GROUPS)]
+        a_codes = keep.tile([P, GROUPS, J], U32, align_bytes=64)
+        a_scales = keep.tile([P, GROUPS, J], U8, align_bytes=64)
+
+        def turn_a(g, half):
+            bank = psum.tile([P, 2, 2, P], F32, tag=("y%d" if half == 0 else "yt%d") % g, name="at_ps")
+            for slot in range(2):
+                pairs = a_raw[g][:, 2 * half + slot, :].bitcast(F32)
+                for u in range(2):
+                    nc.tensor.transpose(bank[:, slot, u, :], pairs[:, u : 2 * P : 2], ident[:])
+            dst = at_grp[g][:, half * 1024 : (half + 1) * 1024].bitcast(F32)
+            nc.scalar.copy(
+                out=dst.rearrange("p (t m u) -> p t m u", t=2, u=2),
+                in_=bank[:].rearrange("p t u m -> p t m u"),
+            )
+
+        def quantize_at(g, half):
+            cols = slice(g * K_PASS + half * 2 * P, g * K_PASS + (half + 1) * 2 * P)
+            quantize(at_codes[:, cols], at_scales[:, cols], at_grp[g][:, half * 1024 : (half + 1) * 1024])
 
         def group_a(g):
             nc.vector.tensor_copy(
@@ -143,102 +158,112 @@ def tile_target_strength_em_biomass_k1_kernel(
                 in_=a_raw[g][:].rearrange("p t (m s) -> p s m t", s=PACK),
             )
 
-        def span_of(c):
-            s = [k for k, (lo, hi) in enumerate(SPANS) if lo <= c * CELLS < hi][0]
-            return s, slice(c * CELLS - SPANS[s][0], (c + 1) * CELLS - SPANS[s][0])
+        def quantize_a(g):
+            quantize(a_codes[:, g, :], a_scales[:, g, :], a_grp[g][:])
 
         p_ps, d_ps, y_ps, yt_ps = {}, {}, {}, {}
         p_sb, inv, sgn, es, gain, r_q, f1_q, f1_grp, r_grp, y_sb, y_grp = {}, {}, {}, {}, {}, {}, {}, {}, {}, {}, {}
         y_codes = {}
         y_scales = keep.tile([P, GROUPS, M], U8, align_bytes=64)
 
-        def predict(c, g):
-            s, cols = span_of(c)
-            p_ps[c, g] = psum.tile([P, PACK, CELLS], F32, tag="p%d" % g, name="p_ps")
-            for t in range(PACK):
-                ch = slice(t * P, (t + 1) * P)
+        def p_banks(c):
+            return GROUPS * PACK * WIDTHS[c] // BANK if 0 <= c < STEPS else 0
+
+        def tiles(c):
+            return WIDTHS[c] // P if 0 <= c < STEPS else 0
+
+        def bank_slots(c, f):
+            per = BANK // WIDTHS[c]
+            g, t0 = divmod(f * per, PACK)
+            return g, t0, per
+
+        def predict(c, f):
+            g, t0, per = bank_slots(c, f)
+            cells = slice(STARTS[c], STARTS[c + 1])
+            p_ps[c, f] = psum.tile([P, per, WIDTHS[c]], F32, tag="p%d" % (f % 2), name="p_ps")
+            for k in range(per):
+                ch = slice(g * K_PASS + (t0 + k) * P, g * K_PASS + (t0 + k + 1) * P)
                 nc.tensor.matmul_mx(
-                    out=p_ps[c, g][:, t, :],
-                    lhsT=at_codes[g][:, ch].bitcast(FP8X4),
-                    lhsT_scale=at_scales[g][:, ch],
-                    rhs=f_codes[s][:, cols].bitcast(FP8X4),
-                    rhs_scale=f_scales[s][:, cols],
+                    out=p_ps[c, f][:, k, :],
+                    lhsT=at_codes[:, ch].bitcast(FP8X4),
+                    lhsT_scale=at_scales[:, ch],
+                    rhs=f_codes[:, cells].bitcast(FP8X4),
+                    rhs_scale=f_scales[:, cells],
                     start=True,
                     stop=True,
                 )
 
-        def add_background(c, g):
-            s, cols = span_of(c)
-            if g == 0:
-                p_sb[c] = work.tile([P, PACK, GROUPS, CELLS], F32, tag="p_sb", name="p_sb")
-            nc.vector.tensor_tensor(out=p_sb[c][:, :, g, :], in0=p_ps[c, g][:], in1=b_raw[s][:, g, :, cols], op=ALU.add)
-
-        def invert(c):
-            flat = p_sb[c][:].rearrange("p t g m -> p (t g m)")
-            inv[c] = work.tile([P, PACK * R_COLS], F32, tag="inv", name="inv")
-            sgn[c] = work.tile([P, PACK * R_COLS], BF16, tag="sgn", name="sgn")
-            nc.scalar.activation(out=inv[c][:, :SIGN_SPLIT], in_=flat[:, :SIGN_SPLIT], func=ACT.Abs_reciprocal_sqrt)
-            nc.scalar.activation(
-                out=inv[c][:, SIGN_SPLIT:], in_=flat[:, SIGN_SPLIT:], func=ACT.Abs_reciprocal_sqrt, scale=0.5
-            )
-            nc.scalar.activation(out=inv[c][:], in_=inv[c][:], func=ACT.Square)
-            nc.scalar.activation(out=sgn[c][:, :SIGN_SPLIT], in_=flat[:, :SIGN_SPLIT], func=ACT.Sign)
-
-        def half_sign(c):
-            flat = p_sb[c][:].rearrange("p t g m -> p (t g m)")
-            nc.vector.tensor_scalar(
-                out=sgn[c][:, SIGN_SPLIT:],
-                in0=flat[:, SIGN_SPLIT:],
-                scalar1=0.0,
-                scalar2=0.5,
-                op0=ALU.is_ge,
-                op1=ALU.subtract,
-            )
-
-        def sign_echo(c):
-            s, cols = span_of(c)
-            es[c] = work.tile([P, PACK, GROUPS, CELLS], BF16, tag="es", name="es")
+        def add_background(c, f):
+            g, t0, per = bank_slots(c, f)
+            s, cols = span_of(STARTS[c], WIDTHS[c])
+            if f == 0:
+                p_sb[c] = work.tile([P, PACK, GROUPS, WIDTHS[c]], F32, tag="p_sb", name="p_sb")
             nc.vector.tensor_tensor(
-                out=es[c][:],
-                in0=e_raw[s][:, :, :, cols].rearrange("p g t m -> p t g m"),
-                in1=sgn[c][:].rearrange("p (t g m) -> p t g m", t=PACK, g=GROUPS),
-                op=ALU.mult,
+                out=p_sb[c][:, t0 : t0 + per, g, :],
+                in0=b_raw[s][:, g, t0 : t0 + per, cols],
+                in1=p_ps[c, f][:],
+                op=ALU.add,
             )
 
-        def ratio_pool(c):
-            r_grp[c] = work.tile([P, R_COLS * PACK], BF16, tag="r_grp", name="r_grp", align_bytes=64)
-            nc.gpsimd.tensor_tensor(
-                out=r_grp[c][:, : POOL_COLS * PACK].rearrange("p (x t) -> p x t", t=PACK),
-                in0=inv[c][:].rearrange("p (t x) -> p x t", t=PACK)[:, :POOL_COLS, :],
-                in1=es[c][:].rearrange("p t g m -> p (g m) t")[:, :POOL_COLS, :],
+        def root(c):
+            inv[c] = work.tile([P, PACK, GROUPS * WIDTHS[c]], F32, tag="inv", name="inv")
+            nc.scalar.activation(
+                out=inv[c][:], in_=p_sb[c][:].rearrange("p t g m -> p t (g m)"), func=ACT.Abs_reciprocal_sqrt
+            )
+
+        def square(c):
+            nc.scalar.activation(out=inv[c][:], in_=inv[c][:], func=ACT.Square)
+
+        def sign(c):
+            sgn[c] = work.tile([P, PACK, GROUPS, WIDTHS[c]], BF16, tag="sgn", name="sgn")
+            nc.scalar.activation(out=sgn[c][:], in_=p_sb[c][:], func=ACT.Sign)
+
+        swap = [keep.tile([P, GROUPS * max(WIDTHS) * PACK], BF16, name="swap%d" % k, align_bytes=64) for k in range(2)]
+
+        def pool_slots(c):
+            banks = p_banks(c + 1) + GROUPS * tiles(c - 2)
+            return min(PACK, (banks - 1) * BANK // (2 * GROUPS * WIDTHS[c]))
+
+        def sign_echo(c, engine, slots):
+            s, cols = span_of(STARTS[c], WIDTHS[c])
+            es[c] = swap[c % 2][:, : GROUPS * WIDTHS[c] * PACK].rearrange("p (t g m) -> p t g m", t=PACK, g=GROUPS)
+            engine.tensor_tensor(
+                out=es[c][:, slots, :, :],
+                in0=e_raw[s][:, :, slots, cols].rearrange("p g t m -> p t g m"),
+                in1=sgn[c][:, slots, :, :],
                 op=ALU.mult,
             )
 
         def ratio(c):
+            r_grp[c] = swap[(c + 1) % 2][:, : GROUPS * WIDTHS[c] * PACK]
             nc.vector.tensor_tensor(
-                out=by_runs_out(r_grp[c][:, POOL_COLS * PACK :]),
-                in0=by_runs_in(inv[c][:].rearrange("p (t x) -> p t x", t=PACK)[:, :, POOL_COLS:]),
-                in1=by_runs_in(es[c][:].rearrange("p t g m -> p t (g m)")[:, :, POOL_COLS:]),
+                out=runs_of_words(r_grp[c]),
+                in0=runs_of_rows(inv[c][:]),
+                in1=runs_of_rows(es[c].rearrange("p t g m -> p t (g m)")),
                 op=ALU.mult,
             )
 
         def quantize_ratio(c):
-            codes = work.tile([P, GROUPS * CELLS], U32, tag="r_codes", name="r_codes", align_bytes=64)
-            scales = work.tile([P, GROUPS * CELLS], U8, tag="r_scales", name="r_scales", align_bytes=64)
-            quantize(codes[:], scales[:], r_grp[c][:])
+            codes = work.tile([P, GROUPS * WIDTHS[c]], U32, tag="r_codes", name="r_codes", align_bytes=64)
+            scales = work.tile([P, GROUPS * WIDTHS[c]], U8, tag="r_scales", name="r_scales", align_bytes=64)
+            quantize(codes[:], scales[:], r_grp[c])
             r_q[c] = (codes, scales)
 
         def back_project(c):
             codes, scales = r_q[c]
-            d_ps[c] = psum.tile([P, PACK, CELLS], F32, tag="d", name="d_ps", bufs=2)
+            width = WIDTHS[c]
+            per = BANK // width
             for t in range(PACK):
+                b, k = divmod(t, per)
+                if k == 0:
+                    d_ps[c, b] = psum.tile([P, per, width], F32, tag="d%d" % ((c + b) % 2), name="d_ps")
                 bins = slice(t * P, (t + 1) * P)
                 for g in range(GROUPS):
-                    cols = slice(g * CELLS, (g + 1) * CELLS)
+                    cols = slice(g * width, (g + 1) * width)
                     nc.tensor.matmul_mx(
-                        out=d_ps[c][:, t, :],
-                        lhsT=a_codes[g][:, bins].bitcast(FP8X4),
-                        lhsT_scale=a_scales[g][:, bins],
+                        out=d_ps[c, b][:, k, :],
+                        lhsT=a_codes[:, g, bins].bitcast(FP8X4),
+                        lhsT_scale=a_scales[:, g, bins],
                         rhs=codes[:, cols].bitcast(FP8X4),
                         rhs_scale=scales[:, cols],
                         start=(g == 0),
@@ -246,155 +271,166 @@ def tile_target_strength_em_biomass_k1_kernel(
                     )
 
         def step_gain(c):
-            gain[c] = work.tile([P, PACK, CELLS], F32, tag="gain", name="gain")
+            gain[c] = work.tile([P, PACK, WIDTHS[c]], F32, tag="gain", name="gain", align_bytes=64)
             for t in range(PACK):
+                b, k = divmod(t, BANK // WIDTHS[c])
                 nc.scalar.activation(
-                    out=gain[c][:, t, :], in_=d_ps[c][:, t, :], func=ACT.Copy, scale=c_f32[:, t : t + 1], bias=1.0
+                    out=gain[c][:, t, :], in_=d_ps[c, b][:, k, :], func=ACT.Copy, scale=c_f32[:, t : t + 1], bias=1.0
                 )
 
         def update(c):
-            s, cols = span_of(c)
-            f1_grp[c] = work.tile([P, CELLS * PACK], BF16, tag="f1_grp", name="f1_grp", align_bytes=64)
+            f1_grp[c] = work.tile([P, WIDTHS[c] * PACK], BF16, tag="f1_grp", name="f1_grp", align_bytes=64)
             nc.vector.tensor_tensor(
-                out=by_runs_out(f1_grp[c][:]),
-                in0=by_runs_in(gain[c][:]),
-                in1=by_runs_out(f_grp[s][:, cols.start * PACK : cols.stop * PACK]),
+                out=runs_of_words(f1_grp[c][:]),
+                in0=runs_of_rows(gain[c][:]),
+                in1=runs_of_words(f_grp[:, STARTS[c] * PACK : STARTS[c + 1] * PACK]),
                 op=ALU.mult,
             )
 
         def quantize_update(c):
-            codes = work.tile([P, CELLS], U32, tag="f1_codes", name="f1_codes", align_bytes=64)
-            scales = work.tile([P, CELLS], U8, tag="f1_scales", name="f1_scales", align_bytes=64)
+            codes = work.tile([P, WIDTHS[c]], U32, tag="f1_codes", name="f1_codes", align_bytes=64)
+            scales = work.tile([P, WIDTHS[c]], U8, tag="f1_scales", name="f1_scales", align_bytes=64)
             quantize(codes[:], scales[:], f1_grp[c][:])
             f1_q[c] = (codes, scales)
 
-        def classify(c):
+        def classify(c, a):
             codes, scales = f1_q[c]
+            cells = slice(a * P, (a + 1) * P)
             for h in range(GROUPS):
-                y_ps[c, h] = psum.tile([P, BANK], F32, tag="y%d" % h, name="y_ps")
+                y_ps[c, a, h] = psum.tile([P, BANK], F32, tag="y%d" % h, name="y_ps")
                 nc.tensor.matmul_mx(
-                    out=y_ps[c, h][:],
-                    lhsT=codes[:].bitcast(FP8X4),
-                    lhsT_scale=scales[:],
+                    out=y_ps[c, a, h][:],
+                    lhsT=codes[:, cells].bitcast(FP8X4),
+                    lhsT_scale=scales[:, cells],
                     rhs=w_words[:, 2 * h * BANK : 2 * (h + 1) * BANK].bitcast(FP4X4),
                     rhs_scale=w_scales[:, h * BANK : (h + 1) * BANK],
                     start=True,
                     stop=True,
                 )
 
-        def weigh(c):
-            y_sb[c] = work.tile([P, N], F32, tag="y_sb", name="y_sb", bufs=3)
+        def weigh(c, a):
+            y_sb[c, a] = work.tile([P, N], F32, tag="y_sb", name="y_sb", bufs=4)
             for h in range(GROUPS):
                 cols = slice(h * BANK, (h + 1) * BANK)
-                nc.vector.tensor_tensor(out=y_sb[c][:, cols], in0=y_ps[c, h][:], in1=v_all[:, cols], op=ALU.mult)
-            nc.sync.dma_start(out=out_0[c * CELLS : (c + 1) * CELLS, :], in_=y_sb[c][:])
+                nc.vector.tensor_tensor(out=y_sb[c, a][:, cols], in0=v_all[:, cols], in1=y_ps[c, a, h][:], op=ALU.mult)
+            first = STARTS[c] + a * P
+            nc.sync.dma_start(out=out_0[first : first + P, :], in_=y_sb[c, a][:])
 
-        def turn_y(c):
+        def turn_y(c, a):
             for g in range(GROUPS):
-                yt_ps[c, g] = psum.tile([P, PACK, CELLS], F32, tag="yt%d" % g, name="yt_ps")
+                yt_ps[c, a, g] = psum.tile([P, PACK, P], F32, tag="yt%d" % g, name="yt_ps")
                 for t in range(PACK):
                     nc.tensor.transpose(
-                        yt_ps[c, g][:, t, :], y_sb[c][:, g * K_PASS + t : (g + 1) * K_PASS : PACK], ident[:]
+                        yt_ps[c, a, g][:, t, :], y_sb[c, a][:, g * K_PASS + t : (g + 1) * K_PASS : PACK], ident[:]
                     )
 
-        def round_y(c):
-            y_grp[c] = work.tile([P, GROUPS, CELLS * PACK], BF16, tag="y_grp", name="y_grp", align_bytes=64)
+        def round_y(c, a):
+            if a == 0:
+                y_grp[c] = work.tile([P, GROUPS, WIDTHS[c] * PACK], BF16, tag="y_grp", name="y_grp", align_bytes=64)
             for g in range(GROUPS):
                 nc.scalar.copy(
-                    out=y_grp[c][:, g, :].rearrange("p (m t) -> p m t", t=PACK),
-                    in_=yt_ps[c, g][:].rearrange("p t m -> p m t"),
+                    out=y_grp[c][:, g, a * K_PASS : (a + 1) * K_PASS].rearrange("p (m t) -> p m t", t=PACK),
+                    in_=yt_ps[c, a, g][:].rearrange("p t m -> p m t"),
                 )
 
         def quantize_y(c):
-            per = PLANE_CELLS // CELLS
-            b, k = divmod(c, per)
-            if k == 0:
+            b, first = divmod(STARTS[c], PLANE_CELLS)
+            if first == 0:
                 y_codes[b] = work.tile([P, GROUPS, PLANE_CELLS], U32, tag="y_codes", name="y_codes", align_bytes=64)
             for g in range(GROUPS):
                 quantize(
-                    y_codes[b][:, g, k * CELLS : (k + 1) * CELLS],
-                    y_scales[:, g, c * CELLS : (c + 1) * CELLS],
+                    y_codes[b][:, g, first : first + WIDTHS[c]],
+                    y_scales[:, g, STARTS[c] : STARTS[c + 1]],
                     y_grp[c][:, g, :],
                 )
-            for lo, hi in PLANE_SPANS:
-                if hi == (c + 1) * CELLS:
+            for lo, hi in WORD_SPANS:
+                if hi == STARTS[c + 1]:
                     nc.sync.dma_start(
                         out=out_1[:, :, lo:hi, :].rearrange("g p m t -> p g (m t)").bitcast(I32),
                         in_=y_codes[b][:, :, lo - b * PLANE_CELLS : hi - b * PLANE_CELLS].bitcast(I32),
                     )
             for lo, hi in SCALE_SPANS:
-                if hi == (c + 1) * CELLS:
+                if hi == STARTS[c + 1]:
                     for q in range(4):
                         nc.sync.dma_start(
                             out=out_2[:, 4 * q : 4 * q + 4, lo:hi].rearrange("g r m -> r g m").bitcast(I32),
                             in_=y_scales[32 * q : 32 * q + 4, :, lo:hi].bitcast(I32),
                         )
 
-        turn_a(0)
-        turn_a(1)
+        turn_a(0, 0)
+        turn_a(0, 1)
         group_f(0)
-        group_a(0)
+        turn_a(1, 0)
+        turn_a(1, 1)
+        quantize_at(0, 0)
         quantize_f(0)
-        quantize(a_codes[0][:], a_scales[0][:], a_grp[0][:])
-        quantize(at_codes[0][:], at_scales[0][:], at_grp[0][:])
+        quantize_at(0, 1)
         predict(0, 0)
-        group_a(1)
-        add_background(0, 0)
-        quantize(at_codes[1][:], at_scales[1][:], at_grp[1][:])
+        group_a(0)
+        quantize_at(1, 0)
+        quantize_at(1, 1)
         predict(0, 1)
-        quantize(a_codes[1][:], a_scales[1][:], a_grp[1][:])
 
         def live(c):
             return 0 <= c < STEPS
 
         for i in range(STEPS + 4):
-            if live(i - 4):
-                round_y(i - 4)
+            part = i + 1 if i + 1 < M // F_PART else None
+            if live(i - 1):
+                sign_echo(i - 1, nc.gpsimd, slice(0, pool_slots(i - 1)))
             if live(i - 2):
                 step_gain(i - 2)
-            if live(i - 1):
-                ratio_pool(i - 1)
-            if live(i):
-                for g in range(GROUPS):
-                    if (i, g) != (0, 0):
-                        add_background(i, g)
-            if live(i - 3):
-                weigh(i - 3)
-            if live(i + 1):
-                for g in range(GROUPS):
-                    predict(i + 1, g)
-            if live(i - 3):
-                turn_y(i - 3)
-            if live(i):
-                invert(i)
+            if part is not None and part not in F_PARTS_ON_VECTOR:
+                group_f(part)
+            for r in range(2):
+                if 2 * r < p_banks(i):
+                    add_background(i, 2 * r)
+                    add_background(i, 2 * r + 1)
+                    if 2 * r + 2 < p_banks(i):
+                        predict(i, 2 * r + 2)
+                        predict(i, 2 * r + 3)
+                if r < tiles(i - 3):
+                    weigh(i - 3, r)
+                    if r + 1 < tiles(i - 3):
+                        classify(i - 3, r + 1)
             if i == 0:
-                group_f(1)
-                group_f(2)
-                quantize_f(1)
+                group_a(1)
+                quantize_a(0)
                 nc.vector.tensor_copy(out=c_f32[:], in_=c_raw[:])
+                quantize_f(1)
+                quantize_a(1)
+            if part is not None and part in F_PARTS_ON_VECTOR:
+                group_f(part)
+            if live(i - 3):
+                turn_y(i - 3, 0)
+            if live(i + 1):
+                predict(i + 1, 0)
+                predict(i + 1, 1)
+            if live(i):
+                root(i)
+            if live(i - 3):
+                round_y(i - 3, 0)
+            if live(i):
+                sign(i)
+            if tiles(i - 3) == 2:
+                turn_y(i - 3, 1)
+            if live(i):
+                square(i)
+            if tiles(i - 3) == 2:
+                round_y(i - 3, 1)
+            if live(i - 1) and pool_slots(i - 1) < PACK:
+                sign_echo(i - 1, nc.vector, slice(pool_slots(i - 1), PACK))
+            if live(i - 2):
+                update(i - 2)
             if live(i - 1):
                 ratio(i - 1)
             if live(i - 2):
-                update(i - 2)
-            if i == 1:
-                quantize_f(2)
+                quantize_update(i - 2)
+                classify(i - 2, 0)
+            if live(i - 4):
+                quantize_y(i - 4)
+            if part is not None and i > 0:
+                quantize_f(part)
             if live(i - 1):
                 quantize_ratio(i - 1)
                 back_project(i - 1)
-            if live(i - 2):
-                quantize_update(i - 2)
-                classify(i - 2)
-            if i == 1:
-                group_f(3)
-            if i == 2:
-                quantize_f(3)
-            if i == 6:
-                group_f(4)
-            if i == 7:
-                quantize_f(4)
-            if live(i):
-                half_sign(i)
-            if live(i - 4):
-                quantize_y(i - 4)
-            if live(i):
-                sign_echo(i)

@@ -22,6 +22,7 @@ K_PASS = P * PACK
 GROUPS = I // K_PASS
 BANK = 512
 RUN = 4
+LONG_RUN = 8
 WIDTHS = [128, 128, 256, 256, 256, 256, 256, 256, 128, 128]
 STARTS = [sum(WIDTHS[:c]) for c in range(len(WIDTHS) + 1)]
 STEPS = len(WIDTHS)
@@ -74,8 +75,8 @@ def tile_target_strength_em_biomass_k1_kernel(
             for g in range(GROUPS):
                 nc.sync.dma_start(out=dst[s][:, g, :, :], in_=rows_of(src, g, lo, hi))
 
-        load_a(0)
         load_f(0)
+        load_a(0)
         load_a(1)
         load_channels(b_raw, reverb, "b_raw", 0)
         load_f(1)
@@ -102,11 +103,11 @@ def tile_target_strength_em_biomass_k1_kernel(
         def quantize(codes, scales, grouped):
             nc.vector.quantize_mx(out=codes.bitcast(FP8X4), scales=scales, in_=grouped)
 
-        def runs_of_words(grouped):
-            return grouped.rearrange("p (c i t) -> p c t i", i=RUN, t=PACK)
+        def runs_of_words(grouped, run=RUN):
+            return grouped.rearrange("p (c i t) -> p c t i", i=run, t=PACK)
 
-        def runs_of_rows(rows):
-            return rows.rearrange("p t (c i) -> p c t i", i=RUN)
+        def runs_of_rows(rows, run=RUN):
+            return rows.rearrange("p t (c i) -> p c t i", i=run)
 
         def span_of(lo, width):
             s = [k for k, (first, last) in enumerate(SPANS) if first <= lo < last][0]
@@ -237,9 +238,9 @@ def tile_target_strength_em_biomass_k1_kernel(
         def ratio(c):
             r_grp[c] = swap[(c + 1) % 2][:, : GROUPS * WIDTHS[c] * PACK]
             nc.vector.tensor_tensor(
-                out=runs_of_words(r_grp[c]),
-                in0=runs_of_rows(inv[c][:]),
-                in1=runs_of_rows(es[c].rearrange("p t g m -> p t (g m)")),
+                out=runs_of_words(r_grp[c], LONG_RUN),
+                in0=runs_of_rows(inv[c][:], LONG_RUN),
+                in1=runs_of_rows(es[c].rearrange("p t g m -> p t (g m)"), LONG_RUN),
                 op=ALU.mult,
             )
 
@@ -280,10 +281,11 @@ def tile_target_strength_em_biomass_k1_kernel(
 
         def update(c):
             f1_grp[c] = work.tile([P, WIDTHS[c] * PACK], BF16, tag="f1_grp", name="f1_grp", align_bytes=64)
+            s, cols = span_of(STARTS[c], WIDTHS[c])
             nc.vector.tensor_tensor(
-                out=runs_of_words(f1_grp[c][:]),
-                in0=runs_of_rows(gain[c][:]),
-                in1=runs_of_words(f_grp[:, STARTS[c] * PACK : STARTS[c + 1] * PACK]),
+                out=runs_of_words(f1_grp[c][:], LONG_RUN),
+                in0=runs_of_rows(gain[c][:], LONG_RUN),
+                in1=runs_of_rows(f_raw[s][:, :, cols], LONG_RUN),
                 op=ALU.mult,
             )
 
@@ -351,22 +353,23 @@ def tile_target_strength_em_biomass_k1_kernel(
                     )
             for lo, hi in SCALE_SPANS:
                 if hi == STARTS[c + 1]:
+                    queue = nc.scalar if hi == M else nc.sync
                     for q in range(4):
-                        nc.sync.dma_start(
+                        queue.dma_start(
                             out=out_2[:, 4 * q : 4 * q + 4, lo:hi].rearrange("g r m -> r g m").bitcast(I32),
                             in_=y_scales[32 * q : 32 * q + 4, :, lo:hi].bitcast(I32),
                         )
 
-        turn_a(0, 0)
-        turn_a(0, 1)
         group_f(0)
-        turn_a(1, 0)
-        turn_a(1, 1)
-        quantize_at(0, 0)
+        for g in range(GROUPS):
+            turn_a(g, 0)
+            turn_a(g, 1)
         quantize_f(0)
+        group_a(0)
+        quantize_at(0, 0)
         quantize_at(0, 1)
         predict(0, 0)
-        group_a(0)
+        quantize_a(0)
         quantize_at(1, 0)
         quantize_at(1, 1)
         predict(0, 1)
@@ -374,7 +377,7 @@ def tile_target_strength_em_biomass_k1_kernel(
         def live(c):
             return 0 <= c < STEPS
 
-        for i in range(STEPS + 4):
+        for i in range(STEPS):
             part = i + 1 if i + 1 < M // F_PART else None
             if live(i - 1):
                 sign_echo(i - 1, nc.gpsimd, slice(0, pool_slots(i - 1)))
@@ -395,7 +398,6 @@ def tile_target_strength_em_biomass_k1_kernel(
                         classify(i - 3, r + 1)
             if i == 0:
                 group_a(1)
-                quantize_a(0)
                 nc.vector.tensor_copy(out=c_f32[:], in_=c_raw[:])
                 quantize_f(1)
                 quantize_a(1)
@@ -434,3 +436,34 @@ def tile_target_strength_em_biomass_k1_kernel(
             if live(i - 1):
                 quantize_ratio(i - 1)
                 back_project(i - 1)
+
+        x, y, z = STEPS - 3, STEPS - 2, STEPS - 1
+        weigh(x, 0)
+        sign_echo(z, nc.vector, slice(0, PACK))
+        classify(x, 1)
+        step_gain(y)
+        weigh(x, 1)
+        update(y)
+        turn_y(x, 0)
+        quantize_update(y)
+        ratio(z)
+        round_y(x, 0)
+        turn_y(x, 1)
+        quantize_ratio(z)
+        classify(y, 0)
+        back_project(z)
+        round_y(x, 1)
+        weigh(y, 0)
+        quantize_y(x - 1)
+        step_gain(z)
+        update(z)
+        turn_y(y, 0)
+        quantize_update(z)
+        classify(z, 0)
+        quantize_y(x)
+        round_y(y, 0)
+        quantize_y(y)
+        weigh(z, 0)
+        turn_y(z, 0)
+        round_y(z, 0)
+        quantize_y(z)

from contextlib import ExitStack

import concourse.mybir as mybir
from concourse.masks import make_identity

M, I, J, N = 2048, 1024, 512, 1024
FLOPS = 2 * (2 * I * J * M + M * J * N)

F32 = mybir.dt.float32
BF16 = mybir.dt.bfloat16
I32 = mybir.dt.int32
U32 = mybir.dt.uint32
U8 = mybir.dt.uint8
FP8X4 = mybir.dt.float8_e4m3fn_x4
FP4X4 = mybir.dt.float4_e2m1fn_x4
ACT = mybir.ActivationFunctionType
ALU = mybir.AluOpType

P = 128
PACK = 4
K_PASS = P * PACK
GROUPS = I // K_PASS
BANK = 512
RUN = 4
LONG_RUN = 8
WIDTHS = [128, 128, 256, 256, 256, 256, 256, 256, 128, 128]
STARTS = [sum(WIDTHS[:c]) for c in range(len(WIDTHS) + 1)]
STEPS = len(WIDTHS)
SPANS = [(0, 256), (256, 512), (512, 1024), (1024, 1536), (1536, 2048)]
F_PART = 256
F_PARTS_ON_VECTOR = (0, 3, 4, 5)
PLANE_CELLS = 512
WORD_SPANS = [(0, 512), (512, 1024), (1024, 1536), (1536, 1920), (1920, 2048)]
SCALE_SPANS = [(0, 1536), (1536, 2048)]


def tile_target_strength_em_biomass_k1_kernel(
    tc, beam, dist, echo, reverb, step, class_words, class_scales, fish_weight, out_0, out_1, out_2
):
    nc = tc.nc

    with ExitStack() as ctx:
        keep = ctx.enter_context(tc.tile_pool(name="keep", bufs=1))
        work = ctx.enter_context(tc.tile_pool(name="work", bufs=2))
        psum = ctx.enter_context(tc.psum_pool(name="psum", bufs=1))
        ctx.enter_context(tc.manual_schedule())

        ident = keep.tile([P, P], F32)
        make_identity(nc, ident[:])
        w_scales = keep.tile([P, N], U8, align_bytes=64)
        nc.gpsimd.memset(w_scales[:].bitcast(I32), 0)

        a_raw = [work.tile([P, PACK, J], BF16, name="a_raw%d" % g, tag="y_sb", bufs=4) for g in range(GROUPS)]
        f_raw = [keep.tile([P, PACK, hi - lo], BF16, name="f_raw%d" % s) for s, (lo, hi) in enumerate(SPANS)]
        b_raw, e_raw = {}, {}
        c_raw = keep.tile([P, PACK], BF16)
        c_f32 = keep.tile([P, PACK], F32)
        v_all = keep.tile([P, N], BF16)
        w_words = keep.tile([P, 2 * N], U8, align_bytes=64)

        def rows_of(src, g, lo, hi):
            return src[g * K_PASS : (g + 1) * K_PASS, lo:hi].rearrange("(p t) m -> p t m", t=PACK)

        def load_f(s):
            nc.sync.dma_start(out=f_raw[s][:], in_=rows_of(dist, 0, *SPANS[s]))

        def load_a(g):
            for half in range(2):
                slots = slice(2 * half, 2 * half + 2)
                nc.sync.dma_start(out=a_raw[g][:, slots, :], in_=rows_of(beam, g, 0, J)[:, slots, :])

        def load_channels(dst, src, tag, s):
            lo, hi = SPANS[s]
            dst[s] = work.tile([P, GROUPS, PACK, hi - lo], BF16, name=tag, tag=tag, bufs=3)
            for g in range(GROUPS):
                nc.sync.dma_start(out=dst[s][:, g, :, :], in_=rows_of(src, g, lo, hi))

        load_f(0)
        load_a(0)
        load_a(1)
        load_channels(b_raw, reverb, "b_raw", 0)
        load_f(1)
        load_channels(e_raw, echo, "e_raw", 0)
        nc.sync.dma_start(out=c_raw[:], in_=step.rearrange("(p t) -> p t", t=PACK))
        load_f(2)
        load_channels(b_raw, reverb, "b_raw", 1)
        load_channels(e_raw, echo, "e_raw", 1)
        nc.sync.dma_start(out=w_words[:].bitcast(I32), in_=class_words[0].bitcast(I32))
        for q in range(4):
            nc.sync.dma_start(
                out=w_scales[32 * q : 32 * q + 4, :].bitcast(I32),
                in_=class_scales[0, 4 * q : 4 * q + 4, :].bitcast(I32),
            )
        load_f(3)
        nc.sync.dma_start(out=v_all[:], in_=fish_weight.partition_broadcast(P))
        load_channels(b_raw, reverb, "b_raw", 2)
        load_channels(e_raw, echo, "e_raw", 2)
        load_f(4)
        for s in (3, 4):
            load_channels(b_raw, reverb, "b_raw", s)
            load_channels(e_raw, echo, "e_raw", s)

        def quantize(codes, scales, grouped):
            nc.vector.quantize_mx(out=codes.bitcast(FP8X4), scales=scales, in_=grouped)

        def runs_of_words(grouped, run=RUN):
            return grouped.rearrange("p (c i t) -> p c t i", i=run, t=PACK)

        def runs_of_rows(rows, run=RUN):
            return rows.rearrange("p t (c i) -> p c t i", i=run)

        def span_of(lo, width):
            s = [k for k, (first, last) in enumerate(SPANS) if first <= lo < last][0]
            return s, slice(lo - SPANS[s][0], lo + width - SPANS[s][0])

        f_grp = keep.tile([P, M * PACK], BF16, align_bytes=64)
        f_codes = keep.tile([P, M], U32, align_bytes=64)
        f_scales = keep.tile([P, M], U8, align_bytes=64)

        def group_f(u):
            s, cols = span_of(u * F_PART, F_PART)
            dst = runs_of_words(f_grp[:, u * F_PART * PACK : (u + 1) * F_PART * PACK])
            src = runs_of_rows(f_raw[s][:, :, cols])
            if u in F_PARTS_ON_VECTOR:
                nc.vector.tensor_copy(out=dst, in_=src)
            else:
                nc.scalar.copy(out=dst, in_=src)

        def quantize_f(u):
            cells = slice(u * F_PART, (u + 1) * F_PART)
            quantize(f_codes[:, cells], f_scales[:, cells], f_grp[:, u * F_PART * PACK : (u + 1) * F_PART * PACK])

        at_grp = [work.tile([P, K_PASS * PACK], BF16, name="at_grp%d" % g, tag="y_grp", align_bytes=64) for g in range(GROUPS)]
        at_codes = keep.tile([P, I], U32, align_bytes=64)
        at_scales = keep.tile([P, I], U8, align_bytes=64)
        a_grp = [work.tile([P, J * PACK], BF16, name="a_grp%d" % g, tag="gain", align_bytes=64) for g in range(GROUPS)]
        a_codes = keep.tile([P, GROUPS, J], U32, align_bytes=64)
        a_scales = keep.tile([P, GROUPS, J], U8, align_bytes=64)

        def turn_a(g, half):
            bank = psum.tile([P, 2, 2, P], F32, tag=("y%d" if half == 0 else "yt%d") % g, name="at_ps")
            for slot in range(2):
                pairs = a_raw[g][:, 2 * half + slot, :].bitcast(F32)
                for u in range(2):
                    nc.tensor.transpose(bank[:, slot, u, :], pairs[:, u : 2 * P : 2], ident[:])
            dst = at_grp[g][:, half * 1024 : (half + 1) * 1024].bitcast(F32)
            nc.scalar.copy(
                out=dst.rearrange("p (t m u) -> p t m u", t=2, u=2),
                in_=bank[:].rearrange("p t u m -> p t m u"),
            )

        def quantize_at(g, half):
            cols = slice(g * K_PASS + half * 2 * P, g * K_PASS + (half + 1) * 2 * P)
            quantize(at_codes[:, cols], at_scales[:, cols], at_grp[g][:, half * 1024 : (half + 1) * 1024])

        def group_a(g):
            nc.vector.tensor_copy(
                out=a_grp[g][:].rearrange("p (s m t) -> p s m t", s=PACK, t=PACK),
                in_=a_raw[g][:].rearrange("p t (m s) -> p s m t", s=PACK),
            )

        def quantize_a(g):
            quantize(a_codes[:, g, :], a_scales[:, g, :], a_grp[g][:])

        p_ps, d_ps, y_ps, yt_ps = {}, {}, {}, {}
        p_sb, inv, sgn, es, gain, r_q, f1_q, f1_grp, r_grp, y_sb, y_grp = {}, {}, {}, {}, {}, {}, {}, {}, {}, {}, {}
        y_codes = {}
        y_scales = keep.tile([P, GROUPS, M], U8, align_bytes=64)

        def p_banks(c):
            return GROUPS * PACK * WIDTHS[c] // BANK if 0 <= c < STEPS else 0

        def tiles(c):
            return WIDTHS[c] // P if 0 <= c < STEPS else 0

        def bank_slots(c, f):
            per = BANK // WIDTHS[c]
            g, t0 = divmod(f * per, PACK)
            return g, t0, per

        def predict(c, f):
            g, t0, per = bank_slots(c, f)
            cells = slice(STARTS[c], STARTS[c + 1])
            p_ps[c, f] = psum.tile([P, per, WIDTHS[c]], F32, tag="p%d" % (f % 2), name="p_ps")
            for k in range(per):
                ch = slice(g * K_PASS + (t0 + k) * P, g * K_PASS + (t0 + k + 1) * P)
                nc.tensor.matmul_mx(
                    out=p_ps[c, f][:, k, :],
                    lhsT=at_codes[:, ch].bitcast(FP8X4),
                    lhsT_scale=at_scales[:, ch],
                    rhs=f_codes[:, cells].bitcast(FP8X4),
                    rhs_scale=f_scales[:, cells],
                    start=True,
                    stop=True,
                )

        def add_background(c, f):
            g, t0, per = bank_slots(c, f)
            s, cols = span_of(STARTS[c], WIDTHS[c])
            if f == 0:
                p_sb[c] = work.tile([P, PACK, GROUPS, WIDTHS[c]], F32, tag="p_sb", name="p_sb")
            nc.vector.tensor_tensor(
                out=p_sb[c][:, t0 : t0 + per, g, :],
                in0=b_raw[s][:, g, t0 : t0 + per, cols],
                in1=p_ps[c, f][:],
                op=ALU.add,
            )

        def root(c):
            inv[c] = work.tile([P, PACK, GROUPS * WIDTHS[c]], F32, tag="inv", name="inv")
            nc.scalar.activation(
                out=inv[c][:], in_=p_sb[c][:].rearrange("p t g m -> p t (g m)"), func=ACT.Abs_reciprocal_sqrt
            )

        def square(c):
            nc.scalar.activation(out=inv[c][:], in_=inv[c][:], func=ACT.Square)

        def sign(c):
            sgn[c] = work.tile([P, PACK, GROUPS, WIDTHS[c]], BF16, tag="sgn", name="sgn")
            nc.scalar.activation(out=sgn[c][:], in_=p_sb[c][:], func=ACT.Sign)

        swap = [keep.tile([P, GROUPS * max(WIDTHS) * PACK], BF16, name="swap%d" % k, align_bytes=64) for k in range(2)]

        def pool_slots(c):
            banks = p_banks(c + 1) + GROUPS * tiles(c - 2)
            return min(PACK, (banks - 1) * BANK // (2 * GROUPS * WIDTHS[c]))

        def sign_echo(c, engine, slots):
            s, cols = span_of(STARTS[c], WIDTHS[c])
            es[c] = swap[c % 2][:, : GROUPS * WIDTHS[c] * PACK].rearrange("p (t g m) -> p t g m", t=PACK, g=GROUPS)
            engine.tensor_tensor(
                out=es[c][:, slots, :, :],
                in0=e_raw[s][:, :, slots, cols].rearrange("p g t m -> p t g m"),
                in1=sgn[c][:, slots, :, :],
                op=ALU.mult,
            )

        def ratio(c):
            r_grp[c] = swap[(c + 1) % 2][:, : GROUPS * WIDTHS[c] * PACK]
            nc.vector.tensor_tensor(
                out=runs_of_words(r_grp[c], LONG_RUN),
                in0=runs_of_rows(inv[c][:], LONG_RUN),
                in1=runs_of_rows(es[c].rearrange("p t g m -> p t (g m)"), LONG_RUN),
                op=ALU.mult,
            )

        def quantize_ratio(c):
            codes = work.tile([P, GROUPS * WIDTHS[c]], U32, tag="r_codes", name="r_codes", align_bytes=64)
            scales = work.tile([P, GROUPS * WIDTHS[c]], U8, tag="r_scales", name="r_scales", align_bytes=64)
            quantize(codes[:], scales[:], r_grp[c])
            r_q[c] = (codes, scales)

        def back_project(c):
            codes, scales = r_q[c]
            width = WIDTHS[c]
            per = BANK // width
            for t in range(PACK):
                b, k = divmod(t, per)
                if k == 0:
                    d_ps[c, b] = psum.tile([P, per, width], F32, tag="d%d" % ((c + b) % 2), name="d_ps")
                bins = slice(t * P, (t + 1) * P)
                for g in range(GROUPS):
                    cols = slice(g * width, (g + 1) * width)
                    nc.tensor.matmul_mx(
                        out=d_ps[c, b][:, k, :],
                        lhsT=a_codes[:, g, bins].bitcast(FP8X4),
                        lhsT_scale=a_scales[:, g, bins],
                        rhs=codes[:, cols].bitcast(FP8X4),
                        rhs_scale=scales[:, cols],
                        start=(g == 0),
                        stop=(g == GROUPS - 1),
                    )

        def step_gain(c):
            gain[c] = work.tile([P, PACK, WIDTHS[c]], F32, tag="gain", name="gain", align_bytes=64)
            for t in range(PACK):
                b, k = divmod(t, BANK // WIDTHS[c])
                nc.scalar.activation(
                    out=gain[c][:, t, :], in_=d_ps[c, b][:, k, :], func=ACT.Copy, scale=c_f32[:, t : t + 1], bias=1.0
                )

        def update(c):
            f1_grp[c] = work.tile([P, WIDTHS[c] * PACK], BF16, tag="f1_grp", name="f1_grp", align_bytes=64)
            s, cols = span_of(STARTS[c], WIDTHS[c])
            nc.vector.tensor_tensor(
                out=runs_of_words(f1_grp[c][:], LONG_RUN),
                in0=runs_of_rows(gain[c][:], LONG_RUN),
                in1=runs_of_rows(f_raw[s][:, :, cols], LONG_RUN),
                op=ALU.mult,
            )

        def quantize_update(c):
            codes = work.tile([P, WIDTHS[c]], U32, tag="f1_codes", name="f1_codes", align_bytes=64)
            scales = work.tile([P, WIDTHS[c]], U8, tag="f1_scales", name="f1_scales", align_bytes=64)
            quantize(codes[:], scales[:], f1_grp[c][:])
            f1_q[c] = (codes, scales)

        def classify(c, a):
            codes, scales = f1_q[c]
            cells = slice(a * P, (a + 1) * P)
            for h in range(GROUPS):
                y_ps[c, a, h] = psum.tile([P, BANK], F32, tag="y%d" % h, name="y_ps")
                nc.tensor.matmul_mx(
                    out=y_ps[c, a, h][:],
                    lhsT=codes[:, cells].bitcast(FP8X4),
                    lhsT_scale=scales[:, cells],
                    rhs=w_words[:, 2 * h * BANK : 2 * (h + 1) * BANK].bitcast(FP4X4),
                    rhs_scale=w_scales[:, h * BANK : (h + 1) * BANK],
                    start=True,
                    stop=True,
                )

        def weigh(c, a):
            y_sb[c, a] = work.tile([P, N], F32, tag="y_sb", name="y_sb", bufs=4)
            for h in range(GROUPS):
                cols = slice(h * BANK, (h + 1) * BANK)
                nc.vector.tensor_tensor(out=y_sb[c, a][:, cols], in0=v_all[:, cols], in1=y_ps[c, a, h][:], op=ALU.mult)
            first = STARTS[c] + a * P
            nc.sync.dma_start(out=out_0[first : first + P, :], in_=y_sb[c, a][:])

        def turn_y(c, a):
            for g in range(GROUPS):
                yt_ps[c, a, g] = psum.tile([P, PACK, P], F32, tag="yt%d" % g, name="yt_ps")
                for t in range(PACK):
                    nc.tensor.transpose(
                        yt_ps[c, a, g][:, t, :], y_sb[c, a][:, g * K_PASS + t : (g + 1) * K_PASS : PACK], ident[:]
                    )

        def round_y(c, a):
            if a == 0:
                y_grp[c] = work.tile([P, GROUPS, WIDTHS[c] * PACK], BF16, tag="y_grp", name="y_grp", align_bytes=64)
            for g in range(GROUPS):
                nc.scalar.copy(
                    out=y_grp[c][:, g, a * K_PASS : (a + 1) * K_PASS].rearrange("p (m t) -> p m t", t=PACK),
                    in_=yt_ps[c, a, g][:].rearrange("p t m -> p m t"),
                )

        def quantize_y(c):
            b, first = divmod(STARTS[c], PLANE_CELLS)
            if first == 0:
                y_codes[b] = work.tile([P, GROUPS, PLANE_CELLS], U32, tag="y_codes", name="y_codes", align_bytes=64)
            for g in range(GROUPS):
                quantize(
                    y_codes[b][:, g, first : first + WIDTHS[c]],
                    y_scales[:, g, STARTS[c] : STARTS[c + 1]],
                    y_grp[c][:, g, :],
                )
            for lo, hi in WORD_SPANS:
                if hi == STARTS[c + 1]:
                    nc.sync.dma_start(
                        out=out_1[:, :, lo:hi, :].rearrange("g p m t -> p g (m t)").bitcast(I32),
                        in_=y_codes[b][:, :, lo - b * PLANE_CELLS : hi - b * PLANE_CELLS].bitcast(I32),
                    )
            for lo, hi in SCALE_SPANS:
                if hi == STARTS[c + 1]:
                    queue = nc.scalar if hi == M else nc.sync
                    for q in range(4):
                        queue.dma_start(
                            out=out_2[:, 4 * q : 4 * q + 4, lo:hi].rearrange("g r m -> r g m").bitcast(I32),
                            in_=y_scales[32 * q : 32 * q + 4, :, lo:hi].bitcast(I32),
                        )

        group_f(0)
        for g in range(GROUPS):
            turn_a(g, 0)
            turn_a(g, 1)
        quantize_f(0)
        group_a(0)
        quantize_at(0, 0)
        quantize_at(0, 1)
        predict(0, 0)
        quantize_a(0)
        quantize_at(1, 0)
        quantize_at(1, 1)
        predict(0, 1)

        def live(c):
            return 0 <= c < STEPS

        for i in range(STEPS):
            part = i + 1 if i + 1 < M // F_PART else None
            if live(i - 1):
                sign_echo(i - 1, nc.gpsimd, slice(0, pool_slots(i - 1)))
            if live(i - 2):
                step_gain(i - 2)
            if part is not None and part not in F_PARTS_ON_VECTOR:
                group_f(part)
            for r in range(2):
                if 2 * r < p_banks(i):
                    add_background(i, 2 * r)
                    add_background(i, 2 * r + 1)
                    if 2 * r + 2 < p_banks(i):
                        predict(i, 2 * r + 2)
                        predict(i, 2 * r + 3)
                if r < tiles(i - 3):
                    weigh(i - 3, r)
                    if r + 1 < tiles(i - 3):
                        classify(i - 3, r + 1)
            if i == 0:
                group_a(1)
                nc.vector.tensor_copy(out=c_f32[:], in_=c_raw[:])
                quantize_f(1)
                quantize_a(1)
            if part is not None and part in F_PARTS_ON_VECTOR:
                group_f(part)
            if live(i - 3):
                turn_y(i - 3, 0)
            if live(i + 1):
                predict(i + 1, 0)
                predict(i + 1, 1)
            if live(i):
                root(i)
            if live(i - 3):
                round_y(i - 3, 0)
            if live(i):
                sign(i)
            if tiles(i - 3) == 2:
                turn_y(i - 3, 1)
            if live(i):
                square(i)
            if tiles(i - 3) == 2:
                round_y(i - 3, 1)
            if live(i - 1) and pool_slots(i - 1) < PACK:
                sign_echo(i - 1, nc.vector, slice(pool_slots(i - 1), PACK))
            if live(i - 2):
                update(i - 2)
            if live(i - 1):
                ratio(i - 1)
            if live(i - 2):
                quantize_update(i - 2)
                classify(i - 2, 0)
            if live(i - 4):
                quantize_y(i - 4)
            if part is not None and i > 0:
                quantize_f(part)
            if live(i - 1):
                quantize_ratio(i - 1)
                back_project(i - 1)

        x, y, z = STEPS - 3, STEPS - 2, STEPS - 1
        weigh(x, 0)
        sign_echo(z, nc.vector, slice(0, PACK))
        classify(x, 1)
        step_gain(y)
        weigh(x, 1)
        update(y)
        turn_y(x, 0)
        quantize_update(y)
        ratio(z)
        round_y(x, 0)
        turn_y(x, 1)
        quantize_ratio(z)
        classify(y, 0)
        back_project(z)
        round_y(x, 1)
        weigh(y, 0)
        quantize_y(x - 1)
        step_gain(z)
        update(z)
        turn_y(y, 0)
        quantize_update(z)
        classify(z, 0)
        quantize_y(x)
        round_y(y, 0)
        quantize_y(y)
        weigh(z, 0)
        turn_y(z, 0)
        round_y(z, 0)
        quantize_y(z)
